import numpy as np
import ml_dtypes


def mxq(x, axis, fmt="e4m3"):
    dtype, down = {"e4m3": (ml_dtypes.float8_e4m3fn, 7), "e5m2": (ml_dtypes.float8_e5m2, 14)}[fmt]
    v = np.moveaxis(np.asarray(x, np.float32).astype(ml_dtypes.bfloat16).astype(np.float64), axis, -1)
    blocks = v.reshape(v.shape[:-1] + (-1, 32))
    amax = np.abs(blocks).max(-1, keepdims=True)
    byte = np.maximum(np.where(amax > 0, np.frexp(amax)[1] - 1 + 127, 0) - down, 1)
    scale = np.exp2(byte - 127.0)
    codes = (blocks / scale).astype(np.float32).astype(dtype).astype(np.float64)
    return np.moveaxis((codes * scale).reshape(v.shape), -1, axis)


WIDE = False


def mx_kscale(k):
    if not WIDE:
        return np.ones(k)
    levels = np.array([30, -30])
    if k % 512:
        return np.exp2(np.random.permutation(np.resize(levels, k // 32))).repeat(32)
    a = np.empty((k // 512, 16))
    for p in range(k // 512):
        a[p, :8] = np.random.permutation(np.resize(levels, 8))
        for g in range(8):
            far = levels[np.abs(levels - a[p, g]) >= 10]
            a[p, g + 8] = far[np.random.randint(len(far))]
    return np.exp2(a.ravel()).repeat(32)


BF16 = ml_dtypes.bfloat16


def bf(x):
    return np.asarray(x, np.float32).astype(BF16)


def f64(x):
    return np.asarray(x).astype(np.float64)


T, R, O, DK, DV = 2048, 1024, 512, 512, 1024


def setup_inputs():
    s, t = mx_kscale(R), mx_kscale(O)
    u = np.concatenate([s, t])
    plain = np.random.standard_normal((T, R))
    tailed = 0.7 * np.random.standard_t(4.0, (T, O))
    latent = np.concatenate([plain, tailed], axis=1) * u
    wk = np.random.standard_normal((DK, R + O)) / np.sqrt(R + O) / u
    wv = np.random.standard_normal((R + O, DV)) / np.sqrt(R + O) / u[:, None]
    return {"latent": bf(latent),
            "wk": bf(wk),
            "wv": bf(wv),
            "bk": bf(0.4 * np.random.standard_normal(DK)),
            "gate": bf(np.random.uniform(0.5, 1.5, T))}


def reference(latent, wk, wv, bk, gate):
    c, k, v = f64(latent), f64(wk), f64(wv)
    a = mxq(c[:, :R], 1, "e4m3")
    h = mxq(c[:, R:], 1, "e5m2")
    keys = (mxq(k[:, :R], 1, "e4m3") @ a.T) + (mxq(k[:, R:], 1, "e4m3") @ h.T)
    keys = keys + f64(bk)[:, None]
    values = (a @ mxq(v[:R], 0, "e4m3")) + (h @ mxq(v[R:], 0, "e4m3"))
    values = values * f64(gate)[:, None]
    return keys, values

@@ -1,0 +1,270 @@
+from contextlib import ExitStack
+
+import concourse.mybir as mybir
+from concourse.masks import make_identity
+
+T, R, O, DK, DV = 2048, 1024, 512, 512, 1024
+K = R + O
+FLOPS = 2 * T * K * (DK + DV)
+
+F32 = mybir.dt.float32
+BF16 = mybir.dt.bfloat16
+U32 = mybir.dt.uint32
+U8 = mybir.dt.uint8
+E4M3 = mybir.dt.float8_e4m3fn_x4
+E5M2 = mybir.dt.float8_e5m2_x4
+IDENTITY = mybir.ActivationFunctionType.Identity
+COPY = mybir.ActivationFunctionType.Copy
+
+P = 128
+W = 512
+PASSES = K // W
+GROUPS = T // W
+HALVES = DV // W
+ROWS = W // P
+DIRECT = []
+OUT_BUFS = 14
+WARM_N = 256
+WARM_PASSES = 8
+
+
+def tile_latent_kv_projection_s2_kernel(tc, latent, wk, wv, bk, gate, out_0, out_1):
+    nc = tc.nc
+    with ExitStack() as ctx:
+        keep = ctx.enter_context(tc.tile_pool(name="keep", bufs=1))
+        stage = ctx.enter_context(tc.tile_pool(name="stage", bufs=1))
+        psum = ctx.enter_context(tc.psum_pool(name="psum", bufs=1))
+        ctx.enter_context(tc.manual_schedule())
+
+        lat_rows = latent.rearrange("(a p i) k -> a p i k", p=P, i=ROWS)
+        wk_rows = wk.rearrange("(p i) k -> p i k", i=ROWS)
+        wv_rows = wv.rearrange("(g p j) n -> g p j n", p=P, j=ROWS)
+        keys_rows = out_0.rearrange("(p i) t -> p i t", i=ROWS)
+        values_rows = out_1.rearrange("(a p i) n -> a p i n", p=P, i=ROWS)
+
+        raw, ordered, grouped, codes, scales = {}, {}, {}, {}, {}
+
+        def label(piece):
+            return "%s_%d_%d" % piece
+
+        def load(piece):
+            kind, a, g = piece
+            if kind == "lat":
+                source = lat_rows[a][:, :, g * W : (g + 1) * W]
+            elif kind == "wk":
+                source = wk_rows[:, :, g * W : (g + 1) * W]
+            else:
+                source = wv_rows[g][:, :, a * W : (a + 1) * W]
+            raw[piece] = keep.tile([P, ROWS, W], BF16, name="raw_" + label(piece), align_bytes=64)
+            nc.sync.dma_start(out=raw[piece][:], in_=source)
+
+        def lat(a):
+            return [("lat", a, g) for g in range(PASSES)]
+
+        def wvh(h):
+            return [("wv", h, g) for g in range(PASSES)]
+
+        wkp = [("wk", 0, g) for g in range(PASSES)]
+        first = [piece for pair in zip(lat(0), wkp) for piece in pair]
+
+        warm = keep.tile([P, 1], F32, name="warm")
+        nc.vector.memset(warm[:], 0.0)
+        nc.scalar.activation(out=warm[:], in_=warm[:], func=IDENTITY)
+        ones = keep.tile([P, 4 * WARM_N], BF16, name="ones", align_bytes=64)
+        nc.vector.memset(ones[:], 1.0)
+        ones_codes = keep.tile([P, WARM_N], U32, name="ones_codes", align_bytes=64)
+        ones_scales = keep.tile([P, WARM_N], U8, name="ones_scales", align_bytes=64)
+        nc.vector.quantize_mx(out=ones_codes[:].bitcast(E4M3), scales=ones_scales[:], in_=ones[:])
+        ident = keep.tile([P, P], F32, name="ident")
+        make_identity(nc, ident[:])
+
+        for piece in first:
+            load(piece)
+        bk_raw = keep.tile([P, ROWS], BF16, name="bk_raw")
+        nc.sync.dma_start(out=bk_raw[:], in_=bk.rearrange("(p i) -> p i", i=ROWS))
+        gate_raw = keep.tile([P, GROUPS, ROWS], BF16, name="gate_raw")
+        nc.sync.dma_start(out=gate_raw[:], in_=gate.rearrange("(a p i) -> p a i", p=P, i=ROWS))
+        for piece in lat(1) + wvh(0) + lat(2) + wvh(1) + lat(3):
+            load(piece)
+
+        bias = keep.tile([P, ROWS], F32, name="bias")
+        gain = keep.tile([P, GROUPS, ROWS], F32, name="gain")
+
+        def bank(b):
+            return psum.tile([P, W], F32, name="bank%d" % b)
+
+        def sort(piece):
+            if piece in DIRECT:
+                return
+            ordered[piece] = stage.tile([P, ROWS, 2, P], F32, name="ordered", bufs=3, align_bytes=64)
+            words = raw[piece][:].bitcast(F32)
+            nc.vector.tensor_copy(out=ordered[piece][:], in_=words.rearrange("p i (w u) -> p i u w", u=2))
+
+        def turn(piece, banks):
+            grouped[piece] = stage.tile([P, 2 * W], F32, name="grouped", bufs=4, align_bytes=64)
+            for half, b in enumerate(banks):
+                xt = bank(b)
+                for n in range(4):
+                    i, u = 2 * half + n // 2, n % 2
+                    if piece in DIRECT:
+                        source = raw[piece][:].bitcast(F32)[:, i, u : 2 * P : 2]
+                    else:
+                        source = ordered[piece][:, i, u, :]
+                    nc.tensor.transpose(xt[:, n * P : (n + 1) * P], source, ident[:])
+                nc.scalar.copy(
+                    out=grouped[piece][:, half * W : (half + 1) * W].rearrange("p (i r u) -> p i r u", i=2, u=2),
+                    in_=xt[:].rearrange("p (i u r) -> p i r u", i=2, u=2),
+                )
+
+        def weave(piece):
+            grouped[piece] = stage.tile([P, 2 * W], F32, name="grouped", bufs=4, align_bytes=64)
+            nc.vector.tensor_copy(
+                out=grouped[piece][:].bitcast(BF16).rearrange("p (c n j) -> p c j n", n=4, j=ROWS),
+                in_=raw[piece][:].rearrange("p j (c n) -> p c j n", n=4),
+            )
+
+        def fmt(piece):
+            return E5M2 if piece[0] == "lat" and piece[2] * W >= R else E4M3
+
+        def quantize(piece):
+            codes[piece] = keep.tile([P, W], U32, name="codes_" + label(piece), align_bytes=64)
+            scales[piece] = keep.tile([P, W], U8, name="scales_" + label(piece), align_bytes=64)
+            nc.vector.quantize_mx(
+                out=codes[piece][:].bitcast(fmt(piece)), scales=scales[piece][:], in_=grouped[piece][:].bitcast(BF16)
+            )
+
+        def mx_pass(acc, fixed, i, moving):
+            cols = slice(i * P, (i + 1) * P)
+            nc.tensor.matmul_mx(
+                out=acc[:],
+                lhsT=codes[fixed][:, cols].bitcast(fmt(fixed)),
+                lhsT_scale=scales[fixed][:, cols],
+                rhs=codes[moving][:].bitcast(fmt(moving)),
+                rhs_scale=scales[moving][:],
+                start=fixed[2] == 0,
+                stop=fixed[2] == PASSES - 1,
+            )
+
+        accs = {}
+
+        def product(job, i, g, b):
+            kind, a, h = job
+            if g == 0:
+                accs[job, i] = bank(b)
+            if kind == "keys":
+                mx_pass(accs[job, i], ("wk", 0, g), i, ("lat", a, g))
+            else:
+                mx_pass(accs[job, i], ("lat", a, g), i, ("wv", h, g))
+            if g == PASSES - 1:
+                finish(job, i)
+
+        results = {}
+        last_job = ("values", GROUPS - 1, HALVES - 1)
+
+        def finish(job, i):
+            kind, a, h = job
+            if i % 2 == 0:
+                results[job] = stage.tile([P, 2, W], F32, name="result", bufs=OUT_BUFS, align_bytes=64)
+            result = results[job]
+            acc = accs[job, i]
+            if kind == "keys":
+                nc.scalar.activation(
+                    out=result[:, i % 2, :].rearrange("p (r j) -> p r j", j=ROWS),
+                    in_=acc[:].rearrange("p (j r) -> p r j", j=ROWS),
+                    func=IDENTITY,
+                    bias=bias[:, i : i + 1],
+                )
+                target = keys_rows[:, :, a * W : (a + 1) * W]
+            else:
+                target = values_rows[a][:, :, h * W : (h + 1) * W]
+                parts = 2 if (job, i) == (last_job, ROWS - 1) else 1
+                for part in range(parts):
+                    cols = slice(part * W // parts, (part + 1) * W // parts)
+                    nc.scalar.activation(
+                        out=result[:, i % 2, cols], in_=acc[:, cols], func=COPY, scale=gain[:, a, i : i + 1]
+                    )
+                    if job == last_job:
+                        nc.sync.dma_start(out=target[:, i, cols], in_=result[:, i % 2, cols])
+            if i % 2 == 1 and job != last_job:
+                nc.sync.dma_start(out=target[:, i - 1 : i + 1, :], in_=result[:])
+
+        def sweep(job, g, b0):
+            for i in range(ROWS):
+                product(job, i, g, b0 + i)
+
+        def whole(job, b0):
+            for i in range(ROWS):
+                for g in range(PASSES):
+                    product(job, i, g, b0 + i)
+
+        l1, l2, l3, v0, v1 = lat(1), lat(2), lat(3), wvh(0), wvh(1)
+
+        idle = bank(0)
+        for n in range(WARM_PASSES):
+            nc.tensor.matmul_mx(
+                out=idle[:, :WARM_N],
+                lhsT=ones_codes[:, :P].bitcast(E4M3),
+                lhsT_scale=ones_scales[:, :P],
+                rhs=ones_codes[:].bitcast(E4M3),
+                rhs_scale=ones_scales[:],
+                start=True,
+                stop=True,
+            )
+
+        head = first + l1
+        for n, piece in enumerate(head):
+            sort(piece)
+            if n >= 2:
+                quantize(head[n - 2])
+            turn(piece, (4, 5) if n % 2 == 0 else (6, 7))
+            if n == 5:
+                nc.vector.tensor_copy(out=bias[:], in_=bk_raw[:])
+                nc.vector.tensor_copy(out=gain[:], in_=gate_raw[:])
+            if n in (3, 5, 7):
+                sweep(("keys", 0, 0), (n - 3) // 2, 0)
+
+        weave(v0[0])
+        quantize(l1[1])
+        sweep(("keys", 1, 0), 0, 0)
+        sweep(("keys", 1, 0), 1, 0)
+        quantize(v0[0])
+        sweep(("values", 0, 0), 0, 4)
+        weave(v0[1])
+        quantize(l1[2])
+        sweep(("keys", 1, 0), 2, 0)
+        quantize(v0[1])
+        sweep(("values", 0, 0), 1, 4)
+        weave(v0[2])
+        sort(l2[0])
+        quantize(v0[2])
+        sort(l2[1])
+        sort(l2[2])
+        turn(l2[0], (0, 1))
+        turn(l2[1], (2, 3))
+        sweep(("values", 0, 0), 2, 4)
+        turn(l2[2], (0, 1))
+        quantize(l2[0])
+        quantize(l2[1])
+        weave(v1[0])
+        quantize(l2[2])
+        quantize(v1[0])
+        for g in range(1, PASSES):
+            weave(v1[g])
+            sort(l3[g - 1])
+            quantize(v1[g])
+        sort(l3[2])
+        whole(("values", 1, 0), 4)
+        whole(("keys", 2, 0), 0)
+        whole(("values", 2, 0), 4)
+        turn(l3[0], (0, 1))
+        turn(l3[1], (2, 3))
+        quantize(l3[0])
+        quantize(l3[1])
+        whole(("values", 0, 1), 4)
+        turn(l3[2], (0, 1))
+        quantize(l3[2])
+        whole(("values", 1, 1), 4)
+        whole(("values", 2, 1), 0)
+        whole(("keys", 3, 0), 4)
+        whole(("values", 3, 0), 0)
+        whole(("values", 3, 1), 4)

@@ -15,6 +15,8 @@ E4M3 = mybir.dt.float8_e4m3fn_x4
 E5M2 = mybir.dt.float8_e5m2_x4
 IDENTITY = mybir.ActivationFunctionType.Identity
 COPY = mybir.ActivationFunctionType.Copy
+ADD = mybir.AluOpType.add
+MULT = mybir.AluOpType.mult
 
 P = 128
 W = 512
@@ -22,10 +24,11 @@ PASSES = K // W
 GROUPS = T // W
 HALVES = DV // W
 ROWS = W // P
-DIRECT = []
 OUT_BUFS = 14
 WARM_N = 256
-WARM_PASSES = 8
+WARM_FIRST = 10
+WARM_BETWEEN = 4
+BANKS = 8
 
 
 def tile_latent_kv_projection_s2_kernel(tc, latent, wk, wv, bk, gate, out_0, out_1):
@@ -80,41 +83,44 @@ def tile_latent_kv_projection_s2_kernel(tc, latent, wk, wv, bk, gate, out_0, out
 
         for piece in first:
             load(piece)
-        bk_raw = keep.tile([P, ROWS], BF16, name="bk_raw")
-        nc.sync.dma_start(out=bk_raw[:], in_=bk.rearrange("(p i) -> p i", i=ROWS))
+        bias = keep.tile([P, ROWS], BF16, name="bias")
+        nc.sync.dma_start(out=bias[:], in_=bk.rearrange("(p i) -> p i", i=ROWS))
+        for piece in lat(1) + wvh(0):
+            load(piece)
         gate_raw = keep.tile([P, GROUPS, ROWS], BF16, name="gate_raw")
         nc.sync.dma_start(out=gate_raw[:], in_=gate.rearrange("(a p i) -> p a i", p=P, i=ROWS))
-        for piece in lat(1) + wvh(0) + lat(2) + wvh(1) + lat(3):
+        for piece in lat(2) + wvh(1):
             load(piece)
+        last_rows = keep.tile([P, ROWS, K], BF16, name="last_rows", align_bytes=64)
+        nc.sync.dma_start(out=last_rows[:], in_=lat_rows[GROUPS - 1])
+        for piece in lat(GROUPS - 1):
+            raw[piece] = last_rows[:, :, piece[2] * W : (piece[2] + 1) * W]
 
-        bias = keep.tile([P, ROWS], F32, name="bias")
         gain = keep.tile([P, GROUPS, ROWS], F32, name="gain")
 
-        def bank(b):
-            return psum.tile([P, W], F32, name="bank%d" % b)
+        free_banks = list(range(BANKS))
 
-        def sort(piece):
-            if piece in DIRECT:
-                return
+        def take_bank():
+            b = free_banks.pop(0)
+            return b, psum.tile([P, W], F32, name="bank%d" % b)
+
+        def sort(piece, copy=nc.vector.tensor_copy):
             ordered[piece] = stage.tile([P, ROWS, 2, P], F32, name="ordered", bufs=3, align_bytes=64)
             words = raw[piece][:].bitcast(F32)
-            nc.vector.tensor_copy(out=ordered[piece][:], in_=words.rearrange("p i (w u) -> p i u w", u=2))
+            copy(out=ordered[piece][:], in_=words.rearrange("p i (w u) -> p i u w", u=2))
 
-        def turn(piece, banks):
+        def turn(piece):
             grouped[piece] = stage.tile([P, 2 * W], F32, name="grouped", bufs=4, align_bytes=64)
-            for half, b in enumerate(banks):
-                xt = bank(b)
+            for half in range(2):
+                b, xt = take_bank()
                 for n in range(4):
                     i, u = 2 * half + n // 2, n % 2
-                    if piece in DIRECT:
-                        source = raw[piece][:].bitcast(F32)[:, i, u : 2 * P : 2]
-                    else:
-                        source = ordered[piece][:, i, u, :]
-                    nc.tensor.transpose(xt[:, n * P : (n + 1) * P], source, ident[:])
+                    nc.tensor.transpose(xt[:, n * P : (n + 1) * P], ordered[piece][:, i, u, :], ident[:])
                 nc.scalar.copy(
                     out=grouped[piece][:, half * W : (half + 1) * W].rearrange("p (i r u) -> p i r u", i=2, u=2),
                     in_=xt[:].rearrange("p (i u r) -> p i r u", i=2, u=2),
                 )
+                free_banks.append(b)
 
         def weave(piece):
             grouped[piece] = stage.tile([P, 2 * W], F32, name="grouped", bufs=4, align_bytes=64)
@@ -145,106 +151,112 @@ def tile_latent_kv_projection_s2_kernel(tc, latent, wk, wv, bk, gate, out_0, out
                 stop=fixed[2] == PASSES - 1,
             )
 
-        accs = {}
-
-        def product(job, i, g, b):
-            kind, a, h = job
-            if g == 0:
-                accs[job, i] = bank(b)
-            if kind == "keys":
-                mx_pass(accs[job, i], ("wk", 0, g), i, ("lat", a, g))
-            else:
-                mx_pass(accs[job, i], ("lat", a, g), i, ("wv", h, g))
-            if g == PASSES - 1:
-                finish(job, i)
-
-        results = {}
+        accs, results = {}, {}
         last_job = ("values", GROUPS - 1, HALVES - 1)
 
-        def finish(job, i):
+        def drain(dst, src, scalar, is_bias, on_vector):
+            if on_vector:
+                nc.vector.tensor_scalar(out=dst, in0=src, scalar1=scalar, scalar2=None, op0=ADD if is_bias else MULT)
+            elif is_bias:
+                nc.scalar.activation(out=dst, in_=src, func=IDENTITY, bias=scalar)
+            else:
+                nc.scalar.activation(out=dst, in_=src, func=COPY, scale=scalar)
+
+        def finish(job, i, shared):
             kind, a, h = job
             if i % 2 == 0:
                 results[job] = stage.tile([P, 2, W], F32, name="result", bufs=OUT_BUFS, align_bytes=64)
             result = results[job]
-            acc = accs[job, i]
+            b, acc = accs[job, i]
+            on_vector = shared and i % 2 == 1
             if kind == "keys":
-                nc.scalar.activation(
-                    out=result[:, i % 2, :].rearrange("p (r j) -> p r j", j=ROWS),
-                    in_=acc[:].rearrange("p (j r) -> p r j", j=ROWS),
-                    func=IDENTITY,
-                    bias=bias[:, i : i + 1],
-                )
+                dst = result[:, i % 2, :].rearrange("p (r j) -> p r j", j=ROWS)
+                drain(dst, acc[:].rearrange("p (j r) -> p r j", j=ROWS), bias[:, i : i + 1], True, on_vector)
                 target = keys_rows[:, :, a * W : (a + 1) * W]
             else:
                 target = values_rows[a][:, :, h * W : (h + 1) * W]
                 parts = 2 if (job, i) == (last_job, ROWS - 1) else 1
                 for part in range(parts):
                     cols = slice(part * W // parts, (part + 1) * W // parts)
-                    nc.scalar.activation(
-                        out=result[:, i % 2, cols], in_=acc[:, cols], func=COPY, scale=gain[:, a, i : i + 1]
-                    )
+                    drain(result[:, i % 2, cols], acc[:, cols], gain[:, a, i : i + 1], False, on_vector)
                     if job == last_job:
                         nc.sync.dma_start(out=target[:, i, cols], in_=result[:, i % 2, cols])
+            free_banks.append(b)
             if i % 2 == 1 and job != last_job:
                 nc.sync.dma_start(out=target[:, i - 1 : i + 1, :], in_=result[:])
 
-        def sweep(job, g, b0):
-            for i in range(ROWS):
-                product(job, i, g, b0 + i)
+        def product(job, i, g, shared):
+            kind, a, h = job
+            if g == 0:
+                accs[job, i] = take_bank()
+            if kind == "keys":
+                mx_pass(accs[job, i][1], ("wk", 0, g), i, ("lat", a, g))
+            else:
+                mx_pass(accs[job, i][1], ("lat", a, g), i, ("wv", h, g))
+            if g == PASSES - 1:
+                finish(job, i, shared)
 
-        def whole(job, b0):
+        def sweep(job, g, tiles=range(ROWS), shared=False):
+            for i in tiles:
+                product(job, i, g, shared)
+
+        def whole(job, shared=False):
             for i in range(ROWS):
                 for g in range(PASSES):
-                    product(job, i, g, b0 + i)
+                    product(job, i, g, shared)
+
+        def keep_warm(passes):
+            b, idle = take_bank()
+            for n in range(passes):
+                nc.tensor.matmul_mx(
+                    out=idle[:, :WARM_N],
+                    lhsT=ones_codes[:, :P].bitcast(E4M3),
+                    lhsT_scale=ones_scales[:, :P],
+                    rhs=ones_codes[:].bitcast(E4M3),
+                    rhs_scale=ones_scales[:],
+                    start=True,
+                    stop=True,
+                )
+            free_banks.append(b)
 
         l1, l2, l3, v0, v1 = lat(1), lat(2), lat(3), wvh(0), wvh(1)
 
-        idle = bank(0)
-        for n in range(WARM_PASSES):
-            nc.tensor.matmul_mx(
-                out=idle[:, :WARM_N],
-                lhsT=ones_codes[:, :P].bitcast(E4M3),
-                lhsT_scale=ones_scales[:, :P],
-                rhs=ones_codes[:].bitcast(E4M3),
-                rhs_scale=ones_scales[:],
-                start=True,
-                stop=True,
-            )
-
+        keep_warm(WARM_FIRST)
         head = first + l1
         for n, piece in enumerate(head):
             sort(piece)
             if n >= 2:
                 quantize(head[n - 2])
-            turn(piece, (4, 5) if n % 2 == 0 else (6, 7))
-            if n == 5:
-                nc.vector.tensor_copy(out=bias[:], in_=bk_raw[:])
-                nc.vector.tensor_copy(out=gain[:], in_=gate_raw[:])
-            if n in (3, 5, 7):
-                sweep(("keys", 0, 0), (n - 3) // 2, 0)
+            turn(piece)
+            if n < 3:
+                keep_warm(WARM_BETWEEN)
+            else:
+                g, half = divmod(n - 3, 2)
+                sweep(("keys", 0, 0), g, (2 * half, 2 * half + 1))
 
         weave(v0[0])
         quantize(l1[1])
-        sweep(("keys", 1, 0), 0, 0)
-        sweep(("keys", 1, 0), 1, 0)
         quantize(v0[0])
-        sweep(("values", 0, 0), 0, 4)
         weave(v0[1])
         quantize(l1[2])
-        sweep(("keys", 1, 0), 2, 0)
         quantize(v0[1])
-        sweep(("values", 0, 0), 1, 4)
         weave(v0[2])
-        sort(l2[0])
-        quantize(v0[2])
+        sweep(("keys", 1, 0), 0)
+        sweep(("keys", 1, 0), 1)
+        sort(l2[0], nc.scalar.copy)
         sort(l2[1])
+        quantize(v0[2])
+        nc.vector.tensor_copy(out=gain[:], in_=gate_raw[:])
         sort(l2[2])
-        turn(l2[0], (0, 1))
-        turn(l2[1], (2, 3))
-        sweep(("values", 0, 0), 2, 4)
-        turn(l2[2], (0, 1))
+        sweep(("values", 0, 0), 0)
+        sweep(("keys", 1, 0), 2)
+        sweep(("values", 0, 0), 1)
+        turn(l2[0])
+        turn(l2[1])
         quantize(l2[0])
+        sweep(("values", 0, 0), 2, shared=True)
         quantize(l2[1])
+        turn(l2[2])
         weave(v1[0])
         quantize(l2[2])
         quantize(v1[0])
@@ -253,18 +265,18 @@ def tile_latent_kv_projection_s2_kernel(tc, latent, wk, wv, bk, gate, out_0, out
             sort(l3[g - 1])
             quantize(v1[g])
         sort(l3[2])
-        whole(("values", 1, 0), 4)
-        whole(("keys", 2, 0), 0)
-        whole(("values", 2, 0), 4)
-        turn(l3[0], (0, 1))
-        turn(l3[1], (2, 3))
+        whole(("values", 1, 0))
+        whole(("keys", 2, 0))
+        whole(("values", 2, 0))
+        turn(l3[0])
+        turn(l3[1])
         quantize(l3[0])
         quantize(l3[1])
-        whole(("values", 0, 1), 4)
-        turn(l3[2], (0, 1))
+        whole(("values", 0, 1))
+        turn(l3[2])
         quantize(l3[2])
-        whole(("values", 1, 1), 4)
-        whole(("values", 2, 1), 0)
-        whole(("keys", 3, 0), 4)
-        whole(("values", 3, 0), 0)
-        whole(("values", 3, 1), 4)
+        whole(("values", 1, 1), shared=True)
+        whole(("values", 2, 1), shared=True)
+        whole(("keys", 3, 0), shared=True)
+        whole(("values", 3, 0), shared=True)
+        whole(("values", 3, 1), shared=True)

@@ -24,11 +24,11 @@ PASSES = K // W
 GROUPS = T // W
 HALVES = DV // W
 ROWS = W // P
-OUT_BUFS = 14
-WARM_N = 256
-WARM_FIRST = 10
-WARM_BETWEEN = 4
 BANKS = 8
+RESULT_BUFS = 14
+WARM_N = 256
+WARM_FIRST = 16
+WARM_BETWEEN = 4
 
 
 def tile_latent_kv_projection_s2_kernel(tc, latent, wk, wv, bk, gate, out_0, out_1):
@@ -47,28 +47,11 @@ def tile_latent_kv_projection_s2_kernel(tc, latent, wk, wv, bk, gate, out_0, out
 
         raw, ordered, grouped, codes, scales = {}, {}, {}, {}, {}
 
-        def label(piece):
-            return "%s_%d_%d" % piece
-
-        def load(piece):
-            kind, a, g = piece
-            if kind == "lat":
-                source = lat_rows[a][:, :, g * W : (g + 1) * W]
-            elif kind == "wk":
-                source = wk_rows[:, :, g * W : (g + 1) * W]
-            else:
-                source = wv_rows[g][:, :, a * W : (a + 1) * W]
-            raw[piece] = keep.tile([P, ROWS, W], BF16, name="raw_" + label(piece), align_bytes=64)
-            nc.sync.dma_start(out=raw[piece][:], in_=source)
-
-        def lat(a):
-            return [("lat", a, g) for g in range(PASSES)]
-
-        def wvh(h):
-            return [("wv", h, g) for g in range(PASSES)]
-
-        wkp = [("wk", 0, g) for g in range(PASSES)]
-        first = [piece for pair in zip(lat(0), wkp) for piece in pair]
+        def load_rows(name):
+            source = wk_rows if name == "wk" else lat_rows[name]
+            for b in range(2):
+                raw[name, b] = keep.tile([P, 2, K], BF16, name="raw_%s_%d" % (name, b), align_bytes=64)
+                nc.sync.dma_start(out=raw[name, b][:], in_=source[:, 2 * b : 2 * b + 2, :])
 
         warm = keep.tile([P, 1], F32, name="warm")
         nc.vector.memset(warm[:], 0.0)
@@ -81,135 +64,81 @@ def tile_latent_kv_projection_s2_kernel(tc, latent, wk, wv, bk, gate, out_0, out
         ident = keep.tile([P, P], F32, name="ident")
         make_identity(nc, ident[:])
 
-        for piece in first:
-            load(piece)
+        load_rows(0)
+        load_rows("wk")
         bias = keep.tile([P, ROWS], BF16, name="bias")
         nc.sync.dma_start(out=bias[:], in_=bk.rearrange("(p i) -> p i", i=ROWS))
-        for piece in lat(1) + wvh(0):
-            load(piece)
+        load_rows(1)
+        for g in range(PASSES):
+            raw["wv", g] = keep.tile([P, ROWS, DV], BF16, name="raw_wv_%d" % g, align_bytes=64)
+            nc.sync.dma_start(out=raw["wv", g][:], in_=wv_rows[g])
         gate_raw = keep.tile([P, GROUPS, ROWS], BF16, name="gate_raw")
         nc.sync.dma_start(out=gate_raw[:], in_=gate.rearrange("(a p i) -> p a i", p=P, i=ROWS))
-        for piece in lat(2) + wvh(1):
-            load(piece)
-        last_rows = keep.tile([P, ROWS, K], BF16, name="last_rows", align_bytes=64)
-        nc.sync.dma_start(out=last_rows[:], in_=lat_rows[GROUPS - 1])
-        for piece in lat(GROUPS - 1):
-            raw[piece] = last_rows[:, :, piece[2] * W : (piece[2] + 1) * W]
+        load_rows(2)
+        load_rows(3)
 
         gain = keep.tile([P, GROUPS, ROWS], F32, name="gain")
 
         free_banks = list(range(BANKS))
 
         def take_bank():
-            b = free_banks.pop(0)
-            return b, psum.tile([P, W], F32, name="bank%d" % b)
+            number = free_banks.pop(0)
+            return number, psum.tile([P, W], F32, name="bank%d" % number)
 
-        def sort(piece, copy=nc.vector.tensor_copy):
-            ordered[piece] = stage.tile([P, ROWS, 2, P], F32, name="ordered", bufs=3, align_bytes=64)
-            words = raw[piece][:].bitcast(F32)
-            copy(out=ordered[piece][:], in_=words.rearrange("p i (w u) -> p i u w", u=2))
+        def sort(name, b):
+            ordered[name, b] = stage.tile([P, 2 * PASSES, 2, P], F32, name="ordered", bufs=3, align_bytes=64)
+            words = raw[name, b][:].rearrange("p i k -> p (i k)").bitcast(F32)
+            nc.vector.tensor_copy(out=ordered[name, b][:], in_=words.rearrange("p (c w u) -> p c u w", w=P, u=2))
 
-        def turn(piece):
-            grouped[piece] = stage.tile([P, 2 * W], F32, name="grouped", bufs=4, align_bytes=64)
-            for half in range(2):
-                b, xt = take_bank()
-                for n in range(4):
-                    i, u = 2 * half + n // 2, n % 2
-                    nc.tensor.transpose(xt[:, n * P : (n + 1) * P], ordered[piece][:, i, u, :], ident[:])
+        def turn(name, b):
+            for g in range(PASSES):
+                number, bank = take_bank()
+                for i in range(2):
+                    for u in range(2):
+                        cols = slice((2 * i + u) * P, (2 * i + u + 1) * P)
+                        nc.tensor.transpose(bank[:, cols], ordered[name, b][:, i * PASSES + g, u, :], ident[:])
+                grouped[name, b, g] = stage.tile([P, W], F32, name="grouped", bufs=6, align_bytes=64)
                 nc.scalar.copy(
-                    out=grouped[piece][:, half * W : (half + 1) * W].rearrange("p (i r u) -> p i r u", i=2, u=2),
-                    in_=xt[:].rearrange("p (i u r) -> p i r u", i=2, u=2),
+                    out=grouped[name, b, g][:].rearrange("p (i r u) -> p i r u", i=2, u=2),
+                    in_=bank[:].rearrange("p (i u r) -> p i r u", i=2, u=2),
                 )
-                free_banks.append(b)
+                free_banks.append(number)
 
-        def weave(piece):
-            grouped[piece] = stage.tile([P, 2 * W], F32, name="grouped", bufs=4, align_bytes=64)
+        def fmt(name, g):
+            return E5M2 if name in range(GROUPS) and g * W >= R else E4M3
+
+        def new_operand(name, g):
+            codes[name, g] = keep.tile([P, W], U32, name="codes_%s_%d" % (name, g), align_bytes=64)
+            scales[name, g] = keep.tile([P, W], U8, name="scales_%s_%d" % (name, g), align_bytes=64)
+
+        def quantize_rows(name, b):
+            cols = slice(2 * b * P, 2 * (b + 1) * P)
+            for g in range(PASSES):
+                if b == 0:
+                    new_operand(name, g)
+                nc.vector.quantize_mx(
+                    out=codes[name, g][:, cols].bitcast(fmt(name, g)),
+                    scales=scales[name, g][:, cols],
+                    in_=grouped[name, b, g][:].bitcast(BF16),
+                )
+
+        def weave(h, g):
+            grouped["wv", h, g] = stage.tile([P, ROWS * W], BF16, name="woven", bufs=2, align_bytes=64)
             nc.vector.tensor_copy(
-                out=grouped[piece][:].bitcast(BF16).rearrange("p (c n j) -> p c j n", n=4, j=ROWS),
-                in_=raw[piece][:].rearrange("p j (c n) -> p c j n", n=4),
+                out=grouped["wv", h, g][:].rearrange("p (c n j) -> p c j n", n=4, j=ROWS),
+                in_=raw["wv", g][:, :, h * W : (h + 1) * W].rearrange("p j (c n) -> p c j n", n=4),
             )
 
-        def fmt(piece):
-            return E5M2 if piece[0] == "lat" and piece[2] * W >= R else E4M3
-
-        def quantize(piece):
-            codes[piece] = keep.tile([P, W], U32, name="codes_" + label(piece), align_bytes=64)
-            scales[piece] = keep.tile([P, W], U8, name="scales_" + label(piece), align_bytes=64)
-            nc.vector.quantize_mx(
-                out=codes[piece][:].bitcast(fmt(piece)), scales=scales[piece][:], in_=grouped[piece][:].bitcast(BF16)
-            )
-
-        def mx_pass(acc, fixed, i, moving):
-            cols = slice(i * P, (i + 1) * P)
-            nc.tensor.matmul_mx(
-                out=acc[:],
-                lhsT=codes[fixed][:, cols].bitcast(fmt(fixed)),
-                lhsT_scale=scales[fixed][:, cols],
-                rhs=codes[moving][:].bitcast(fmt(moving)),
-                rhs_scale=scales[moving][:],
-                start=fixed[2] == 0,
-                stop=fixed[2] == PASSES - 1,
-            )
-
-        accs, results = {}, {}
-        last_job = ("values", GROUPS - 1, HALVES - 1)
-
-        def drain(dst, src, scalar, is_bias, on_vector):
-            if on_vector:
-                nc.vector.tensor_scalar(out=dst, in0=src, scalar1=scalar, scalar2=None, op0=ADD if is_bias else MULT)
-            elif is_bias:
-                nc.scalar.activation(out=dst, in_=src, func=IDENTITY, bias=scalar)
-            else:
-                nc.scalar.activation(out=dst, in_=src, func=COPY, scale=scalar)
-
-        def finish(job, i, shared):
-            kind, a, h = job
-            if i % 2 == 0:
-                results[job] = stage.tile([P, 2, W], F32, name="result", bufs=OUT_BUFS, align_bytes=64)
-            result = results[job]
-            b, acc = accs[job, i]
-            on_vector = shared and i % 2 == 1
-            if kind == "keys":
-                dst = result[:, i % 2, :].rearrange("p (r j) -> p r j", j=ROWS)
-                drain(dst, acc[:].rearrange("p (j r) -> p r j", j=ROWS), bias[:, i : i + 1], True, on_vector)
-                target = keys_rows[:, :, a * W : (a + 1) * W]
-            else:
-                target = values_rows[a][:, :, h * W : (h + 1) * W]
-                parts = 2 if (job, i) == (last_job, ROWS - 1) else 1
-                for part in range(parts):
-                    cols = slice(part * W // parts, (part + 1) * W // parts)
-                    drain(result[:, i % 2, cols], acc[:, cols], gain[:, a, i : i + 1], False, on_vector)
-                    if job == last_job:
-                        nc.sync.dma_start(out=target[:, i, cols], in_=result[:, i % 2, cols])
-            free_banks.append(b)
-            if i % 2 == 1 and job != last_job:
-                nc.sync.dma_start(out=target[:, i - 1 : i + 1, :], in_=result[:])
-
-        def product(job, i, g, shared):
-            kind, a, h = job
-            if g == 0:
-                accs[job, i] = take_bank()
-            if kind == "keys":
-                mx_pass(accs[job, i][1], ("wk", 0, g), i, ("lat", a, g))
-            else:
-                mx_pass(accs[job, i][1], ("lat", a, g), i, ("wv", h, g))
-            if g == PASSES - 1:
-                finish(job, i, shared)
-
-        def sweep(job, g, tiles=range(ROWS), shared=False):
-            for i in tiles:
-                product(job, i, g, shared)
-
-        def whole(job, shared=False):
-            for i in range(ROWS):
-                for g in range(PASSES):
-                    product(job, i, g, shared)
+        def quantize_wv(h, g):
+            name = "wv%d" % h
+            new_operand(name, g)
+            nc.vector.quantize_mx(out=codes[name, g][:].bitcast(E4M3), scales=scales[name, g][:], in_=grouped["wv", h, g][:])
 
         def keep_warm(passes):
-            b, idle = take_bank()
+            number, bank = take_bank()
             for n in range(passes):
                 nc.tensor.matmul_mx(
-                    out=idle[:, :WARM_N],
+                    out=bank[:, :WARM_N],
                     lhsT=ones_codes[:, :P].bitcast(E4M3),
                     lhsT_scale=ones_scales[:, :P],
                     rhs=ones_codes[:].bitcast(E4M3),
@@ -217,66 +146,142 @@ def tile_latent_kv_projection_s2_kernel(tc, latent, wk, wv, bk, gate, out_0, out
                     start=True,
                     stop=True,
                 )
-            free_banks.append(b)
+            free_banks.append(number)
 
-        l1, l2, l3, v0, v1 = lat(1), lat(2), lat(3), wvh(0), wvh(1)
+        def mx_pass(bank, fixed, i, moving, g):
+            cols = slice(i * P, (i + 1) * P)
+            nc.tensor.matmul_mx(
+                out=bank[:],
+                lhsT=codes[fixed, g][:, cols].bitcast(fmt(fixed, g)),
+                lhsT_scale=scales[fixed, g][:, cols],
+                rhs=codes[moving, g][:].bitcast(fmt(moving, g)),
+                rhs_scale=scales[moving, g][:],
+                start=g == 0,
+                stop=g == PASSES - 1,
+            )
+
+        def new_result():
+            return stage.tile([P, 2, W], F32, name="result", bufs=RESULT_BUFS, align_bytes=64)
+
+        def keys_tile(a, i, dst, on_vector):
+            number, bank = take_bank()
+            for g in range(PASSES):
+                mx_pass(bank, "wk", i, a, g)
+            dst = dst.rearrange("p (r j) -> p r j", j=ROWS)
+            src = bank[:].rearrange("p (j r) -> p r j", j=ROWS)
+            if on_vector:
+                nc.vector.tensor_scalar(out=dst, in0=src, scalar1=bias[:, i : i + 1], scalar2=None, op0=ADD)
+            else:
+                nc.scalar.activation(out=dst, in_=src, func=IDENTITY, bias=bias[:, i : i + 1])
+            free_banks.append(number)
+
+        def gate_values(a, i, dst, src, on_vector):
+            if on_vector:
+                nc.vector.tensor_scalar(out=dst, in0=src, scalar1=gain[:, a, i : i + 1], scalar2=None, op0=MULT)
+            else:
+                nc.scalar.activation(out=dst, in_=src, func=COPY, scale=gain[:, a, i : i + 1])
+
+        def values_tile(a, i, h, dst, on_vector):
+            number, bank = take_bank()
+            for g in range(PASSES):
+                mx_pass(bank, a, i, "wv%d" % h, g)
+            gate_values(a, i, dst, bank[:], on_vector)
+            free_banks.append(number)
+
+        def keys_pair(a, b, shared=False):
+            result = new_result()
+            for i in range(2):
+                keys_tile(a, 2 * b + i, result[:, i, :], shared and i == 1)
+            nc.sync.dma_start(out=keys_rows[:, 2 * b : 2 * b + 2, a * W : (a + 1) * W], in_=result[:])
+
+        def values_pair(a, b, h, shared=False):
+            result = new_result()
+            for i in range(2):
+                values_tile(a, 2 * b + i, h, result[:, i, :], shared and i == 1)
+            nc.sync.dma_start(out=values_rows[a][:, 2 * b : 2 * b + 2, h * W : (h + 1) * W], in_=result[:])
 
         keep_warm(WARM_FIRST)
-        head = first + l1
-        for n, piece in enumerate(head):
-            sort(piece)
+        head = [(name, b) for name in (0, "wk", 1) for b in range(2)]
+        wide = [new_result() for i in range(ROWS)]
+        for n, (name, b) in enumerate(head):
+            sort(name, b)
             if n >= 2:
-                quantize(head[n - 2])
-            turn(piece)
-            if n < 3:
+                quantize_rows(*head[n - 2])
+            if n in (1, 2, 3, 4):
                 keep_warm(WARM_BETWEEN)
-            else:
-                g, half = divmod(n - 3, 2)
-                sweep(("keys", 0, 0), g, (2 * half, 2 * half + 1))
+            turn(name, b)
+            if name == 1:
+                for i in (2 * b, 2 * b + 1):
+                    keys_tile(0, i, wide[i][:, 0, :], False)
 
-        weave(v0[0])
-        quantize(l1[1])
-        quantize(v0[0])
-        weave(v0[1])
-        quantize(l1[2])
-        quantize(v0[1])
-        weave(v0[2])
-        sweep(("keys", 1, 0), 0)
-        sweep(("keys", 1, 0), 1)
-        sort(l2[0], nc.scalar.copy)
-        sort(l2[1])
-        quantize(v0[2])
+        quantize_rows(1, 0)
+        weave(0, 0)
+        quantize_rows(1, 1)
+        quantize_wv(0, 0)
+        weave(0, 1)
+        for i in range(ROWS):
+            keys_tile(1, i, wide[i][:, 1, :], False)
+            nc.sync.dma_start(out=keys_rows[:, i, : 2 * W], in_=wide[i][:].rearrange("p a t -> p (a t)"))
+        quantize_wv(0, 1)
+        weave(0, 2)
+        sort(2, 0)
+        quantize_wv(0, 2)
         nc.vector.tensor_copy(out=gain[:], in_=gate_raw[:])
-        sort(l2[2])
-        sweep(("values", 0, 0), 0)
-        sweep(("keys", 1, 0), 2)
-        sweep(("values", 0, 0), 1)
-        turn(l2[0])
-        turn(l2[1])
-        quantize(l2[0])
-        sweep(("values", 0, 0), 2, shared=True)
-        quantize(l2[1])
-        turn(l2[2])
-        weave(v1[0])
-        quantize(l2[2])
-        quantize(v1[0])
+        sort(2, 1)
+
+        held = [take_bank() for i in range(ROWS)]
+        for g in range(PASSES - 1):
+            for i in range(ROWS):
+                mx_pass(held[i][1], 0, i, "wv0", g)
+        turn(2, 0)
+        quantize_rows(2, 0)
+        for b in range(2):
+            result = new_result()
+            for i in range(2):
+                number, bank = held[2 * b + i]
+                mx_pass(bank, 0, 2 * b + i, "wv0", PASSES - 1)
+                gate_values(0, 2 * b + i, result[:, i, :], bank[:], i == 1)
+                free_banks.append(number)
+            nc.sync.dma_start(out=values_rows[0][:, 2 * b : 2 * b + 2, :W], in_=result[:])
+        turn(2, 1)
+        weave(1, 0)
+        quantize_rows(2, 1)
+        quantize_wv(1, 0)
         for g in range(1, PASSES):
-            weave(v1[g])
-            sort(l3[g - 1])
-            quantize(v1[g])
-        sort(l3[2])
-        whole(("values", 1, 0))
-        whole(("keys", 2, 0))
-        whole(("values", 2, 0))
-        turn(l3[0])
-        turn(l3[1])
-        quantize(l3[0])
-        quantize(l3[1])
-        whole(("values", 0, 1))
-        turn(l3[2])
-        quantize(l3[2])
-        whole(("values", 1, 1), shared=True)
-        whole(("values", 2, 1), shared=True)
-        whole(("keys", 3, 0), shared=True)
-        whole(("values", 3, 0), shared=True)
-        whole(("values", 3, 1), shared=True)
+            weave(1, g)
+            sort(3, g - 1)
+            quantize_wv(1, g)
+
+        for b in range(2):
+            values_pair(1, b, 0)
+        for b in range(2):
+            keys_pair(2, b)
+        for b in range(2):
+            values_pair(2, b, 0)
+            turn(3, b)
+        for b in range(2):
+            quantize_rows(3, b)
+        for a in range(GROUPS - 1):
+            for b in range(2):
+                values_pair(a, b, 1, shared=True)
+        for b in range(2):
+            keys_pair(3, b, shared=True)
+
+        last = GROUPS - 1
+        for i in range(2):
+            result = new_result()
+            for h in range(HALVES):
+                values_tile(last, i, h, result[:, h, :], h == 1)
+            nc.sync.dma_start(out=values_rows[last][:, i, :], in_=result[:].rearrange("p h n -> p (h n)"))
+        for i in range(2, ROWS):
+            result = new_result()
+            for h in range(HALVES):
+                number, bank = take_bank()
+                for g in range(PASSES):
+                    mx_pass(bank, last, i, "wv%d" % h, g)
+                parts = 2 if (i, h) == (ROWS - 1, HALVES - 1) else 1
+                for part in range(parts):
+                    cols = slice(part * W // parts, (part + 1) * W // parts)
+                    gate_values(last, i, result[:, h, cols], bank[:, cols], h == 1)
+                    nc.sync.dma_start(out=values_rows[last][:, i, h * W : (h + 1) * W][:, cols], in_=result[:, h, cols])
+                free_banks.append(number)

from contextlib import ExitStack

import concourse.mybir as mybir
from concourse.masks import make_identity

T, R, O, DK, DV = 2048, 1024, 512, 512, 1024
K = R + O
FLOPS = 2 * T * K * (DK + DV)

F32 = mybir.dt.float32
BF16 = mybir.dt.bfloat16
U32 = mybir.dt.uint32
U8 = mybir.dt.uint8
E4M3 = mybir.dt.float8_e4m3fn_x4
E5M2 = mybir.dt.float8_e5m2_x4
IDENTITY = mybir.ActivationFunctionType.Identity
COPY = mybir.ActivationFunctionType.Copy
ADD = mybir.AluOpType.add
MULT = mybir.AluOpType.mult

P = 128
W = 512
PASSES = K // W
GROUPS = T // W
HALVES = DV // W
ROWS = W // P
BANKS = 8
RESULT_BUFS = 14
WARM_N = 256
WARM_FIRST = 16
WARM_BETWEEN = 4


def tile_latent_kv_projection_s2_kernel(tc, latent, wk, wv, bk, gate, out_0, out_1):
    nc = tc.nc
    with ExitStack() as ctx:
        keep = ctx.enter_context(tc.tile_pool(name="keep", bufs=1))
        stage = ctx.enter_context(tc.tile_pool(name="stage", bufs=1))
        psum = ctx.enter_context(tc.psum_pool(name="psum", bufs=1))
        ctx.enter_context(tc.manual_schedule())

        lat_rows = latent.rearrange("(a p i) k -> a p i k", p=P, i=ROWS)
        wk_rows = wk.rearrange("(p i) k -> p i k", i=ROWS)
        wv_rows = wv.rearrange("(g p j) n -> g p j n", p=P, j=ROWS)
        keys_rows = out_0.rearrange("(p i) t -> p i t", i=ROWS)
        values_rows = out_1.rearrange("(a p i) n -> a p i n", p=P, i=ROWS)

        raw, ordered, grouped, codes, scales = {}, {}, {}, {}, {}

        def load_rows(name):
            source = wk_rows if name == "wk" else lat_rows[name]
            for b in range(2):
                raw[name, b] = keep.tile([P, 2, K], BF16, name="raw_%s_%d" % (name, b), align_bytes=64)
                nc.sync.dma_start(out=raw[name, b][:], in_=source[:, 2 * b : 2 * b + 2, :])

        warm = keep.tile([P, 1], F32, name="warm")
        nc.vector.memset(warm[:], 0.0)
        nc.scalar.activation(out=warm[:], in_=warm[:], func=IDENTITY)
        ones = keep.tile([P, 4 * WARM_N], BF16, name="ones", align_bytes=64)
        nc.vector.memset(ones[:], 1.0)
        ones_codes = keep.tile([P, WARM_N], U32, name="ones_codes", align_bytes=64)
        ones_scales = keep.tile([P, WARM_N], U8, name="ones_scales", align_bytes=64)
        nc.vector.quantize_mx(out=ones_codes[:].bitcast(E4M3), scales=ones_scales[:], in_=ones[:])
        ident = keep.tile([P, P], F32, name="ident")
        make_identity(nc, ident[:])

        load_rows(0)
        load_rows("wk")
        bias = keep.tile([P, ROWS], BF16, name="bias")
        nc.sync.dma_start(out=bias[:], in_=bk.rearrange("(p i) -> p i", i=ROWS))
        load_rows(1)
        for g in range(PASSES):
            raw["wv", g] = keep.tile([P, ROWS, DV], BF16, name="raw_wv_%d" % g, align_bytes=64)
            nc.sync.dma_start(out=raw["wv", g][:], in_=wv_rows[g])
        gate_raw = keep.tile([P, GROUPS, ROWS], BF16, name="gate_raw")
        nc.sync.dma_start(out=gate_raw[:], in_=gate.rearrange("(a p i) -> p a i", p=P, i=ROWS))
        load_rows(2)
        load_rows(3)

        gain = keep.tile([P, GROUPS, ROWS], F32, name="gain")

        free_banks = list(range(BANKS))

        def take_bank():
            number = free_banks.pop(0)
            return number, psum.tile([P, W], F32, name="bank%d" % number)

        def sort(name, b):
            ordered[name, b] = stage.tile([P, 2 * PASSES, 2, P], F32, name="ordered", bufs=3, align_bytes=64)
            words = raw[name, b][:].rearrange("p i k -> p (i k)").bitcast(F32)
            nc.vector.tensor_copy(out=ordered[name, b][:], in_=words.rearrange("p (c w u) -> p c u w", w=P, u=2))

        def turn(name, b):
            for g in range(PASSES):
                number, bank = take_bank()
                for i in range(2):
                    for u in range(2):
                        cols = slice((2 * i + u) * P, (2 * i + u + 1) * P)
                        nc.tensor.transpose(bank[:, cols], ordered[name, b][:, i * PASSES + g, u, :], ident[:])
                grouped[name, b, g] = stage.tile([P, W], F32, name="grouped", bufs=6, align_bytes=64)
                nc.scalar.copy(
                    out=grouped[name, b, g][:].rearrange("p (i r u) -> p i r u", i=2, u=2),
                    in_=bank[:].rearrange("p (i u r) -> p i r u", i=2, u=2),
                )
                free_banks.append(number)

        def fmt(name, g):
            return E5M2 if name in range(GROUPS) and g * W >= R else E4M3

        def new_operand(name, g):
            codes[name, g] = keep.tile([P, W], U32, name="codes_%s_%d" % (name, g), align_bytes=64)
            scales[name, g] = keep.tile([P, W], U8, name="scales_%s_%d" % (name, g), align_bytes=64)

        def quantize_rows(name, b):
            cols = slice(2 * b * P, 2 * (b + 1) * P)
            for g in range(PASSES):
                if b == 0:
                    new_operand(name, g)
                nc.vector.quantize_mx(
                    out=codes[name, g][:, cols].bitcast(fmt(name, g)),
                    scales=scales[name, g][:, cols],
                    in_=grouped[name, b, g][:].bitcast(BF16),
                )

        def weave(h, g):
            grouped["wv", h, g] = stage.tile([P, ROWS * W], BF16, name="woven", bufs=2, align_bytes=64)
            nc.vector.tensor_copy(
                out=grouped["wv", h, g][:].rearrange("p (c n j) -> p c j n", n=4, j=ROWS),
                in_=raw["wv", g][:, :, h * W : (h + 1) * W].rearrange("p j (c n) -> p c j n", n=4),
            )

        def quantize_wv(h, g):
            name = "wv%d" % h
            new_operand(name, g)
            nc.vector.quantize_mx(out=codes[name, g][:].bitcast(E4M3), scales=scales[name, g][:], in_=grouped["wv", h, g][:])

        def keep_warm(passes):
            number, bank = take_bank()
            for n in range(passes):
                nc.tensor.matmul_mx(
                    out=bank[:, :WARM_N],
                    lhsT=ones_codes[:, :P].bitcast(E4M3),
                    lhsT_scale=ones_scales[:, :P],
                    rhs=ones_codes[:].bitcast(E4M3),
                    rhs_scale=ones_scales[:],
                    start=True,
                    stop=True,
                )
            free_banks.append(number)

        def mx_pass(bank, fixed, i, moving, g):
            cols = slice(i * P, (i + 1) * P)
            nc.tensor.matmul_mx(
                out=bank[:],
                lhsT=codes[fixed, g][:, cols].bitcast(fmt(fixed, g)),
                lhsT_scale=scales[fixed, g][:, cols],
                rhs=codes[moving, g][:].bitcast(fmt(moving, g)),
                rhs_scale=scales[moving, g][:],
                start=g == 0,
                stop=g == PASSES - 1,
            )

        def new_result():
            return stage.tile([P, 2, W], F32, name="result", bufs=RESULT_BUFS, align_bytes=64)

        def keys_tile(a, i, dst, on_vector):
            number, bank = take_bank()
            for g in range(PASSES):
                mx_pass(bank, "wk", i, a, g)
            dst = dst.rearrange("p (r j) -> p r j", j=ROWS)
            src = bank[:].rearrange("p (j r) -> p r j", j=ROWS)
            if on_vector:
                nc.vector.tensor_scalar(out=dst, in0=src, scalar1=bias[:, i : i + 1], scalar2=None, op0=ADD)
            else:
                nc.scalar.activation(out=dst, in_=src, func=IDENTITY, bias=bias[:, i : i + 1])
            free_banks.append(number)

        def gate_values(a, i, dst, src, on_vector):
            if on_vector:
                nc.vector.tensor_scalar(out=dst, in0=src, scalar1=gain[:, a, i : i + 1], scalar2=None, op0=MULT)
            else:
                nc.scalar.activation(out=dst, in_=src, func=COPY, scale=gain[:, a, i : i + 1])

        def values_tile(a, i, h, dst, on_vector):
            number, bank = take_bank()
            for g in range(PASSES):
                mx_pass(bank, a, i, "wv%d" % h, g)
            gate_values(a, i, dst, bank[:], on_vector)
            free_banks.append(number)

        def keys_pair(a, b, shared=False):
            result = new_result()
            for i in range(2):
                keys_tile(a, 2 * b + i, result[:, i, :], shared and i == 1)
            nc.sync.dma_start(out=keys_rows[:, 2 * b : 2 * b + 2, a * W : (a + 1) * W], in_=result[:])

        def values_pair(a, b, h, shared=False):
            result = new_result()
            for i in range(2):
                values_tile(a, 2 * b + i, h, result[:, i, :], shared and i == 1)
            nc.sync.dma_start(out=values_rows[a][:, 2 * b : 2 * b + 2, h * W : (h + 1) * W], in_=result[:])

        keep_warm(WARM_FIRST)
        head = [(name, b) for name in (0, "wk", 1) for b in range(2)]
        wide = [new_result() for i in range(ROWS)]
        for n, (name, b) in enumerate(head):
            sort(name, b)
            if n >= 2:
                quantize_rows(*head[n - 2])
            if n in (1, 2, 3, 4):
                keep_warm(WARM_BETWEEN)
            turn(name, b)
            if name == 1:
                for i in (2 * b, 2 * b + 1):
                    keys_tile(0, i, wide[i][:, 0, :], False)

        quantize_rows(1, 0)
        weave(0, 0)
        quantize_rows(1, 1)
        quantize_wv(0, 0)
        weave(0, 1)
        for i in range(ROWS):
            keys_tile(1, i, wide[i][:, 1, :], False)
            nc.sync.dma_start(out=keys_rows[:, i, : 2 * W], in_=wide[i][:].rearrange("p a t -> p (a t)"))
        quantize_wv(0, 1)
        weave(0, 2)
        sort(2, 0)
        quantize_wv(0, 2)
        nc.vector.tensor_copy(out=gain[:], in_=gate_raw[:])
        sort(2, 1)

        held = [take_bank() for i in range(ROWS)]
        for g in range(PASSES - 1):
            for i in range(ROWS):
                mx_pass(held[i][1], 0, i, "wv0", g)
        turn(2, 0)
        quantize_rows(2, 0)
        for b in range(2):
            result = new_result()
            for i in range(2):
                number, bank = held[2 * b + i]
                mx_pass(bank, 0, 2 * b + i, "wv0", PASSES - 1)
                gate_values(0, 2 * b + i, result[:, i, :], bank[:], i == 1)
                free_banks.append(number)
            nc.sync.dma_start(out=values_rows[0][:, 2 * b : 2 * b + 2, :W], in_=result[:])
        turn(2, 1)
        weave(1, 0)
        quantize_rows(2, 1)
        quantize_wv(1, 0)
        for g in range(1, PASSES):
            weave(1, g)
            sort(3, g - 1)
            quantize_wv(1, g)

        for b in range(2):
            values_pair(1, b, 0)
        for b in range(2):
            keys_pair(2, b)
        for b in range(2):
            values_pair(2, b, 0)
            turn(3, b)
        for b in range(2):
            quantize_rows(3, b)
        for a in range(GROUPS - 1):
            for b in range(2):
                values_pair(a, b, 1, shared=True)
        for b in range(2):
            keys_pair(3, b, shared=True)

        last = GROUPS - 1
        for i in range(2):
            result = new_result()
            for h in range(HALVES):
                values_tile(last, i, h, result[:, h, :], h == 1)
            nc.sync.dma_start(out=values_rows[last][:, i, :], in_=result[:].rearrange("p h n -> p (h n)"))
        for i in range(2, ROWS):
            result = new_result()
            for h in range(HALVES):
                number, bank = take_bank()
                for g in range(PASSES):
                    mx_pass(bank, last, i, "wv%d" % h, g)
                parts = 2 if (i, h) == (ROWS - 1, HALVES - 1) else 1
                for part in range(parts):
                    cols = slice(part * W // parts, (part + 1) * W // parts)
                    gate_values(last, i, result[:, h, cols], bank[:, cols], h == 1)
                    nc.sync.dma_start(out=values_rows[last][:, i, h * W : (h + 1) * W][:, cols], in_=result[:, h, cols])
                free_banks.append(number)
